import numpy as np
import ml_dtypes


def mxq(x, axis, fmt="e4m3"):
    dtype, down = {"e4m3": (ml_dtypes.float8_e4m3fn, 7), "e5m2": (ml_dtypes.float8_e5m2, 14)}[fmt]
    v = np.moveaxis(np.asarray(x, np.float32).astype(ml_dtypes.bfloat16).astype(np.float64), axis, -1)
    blocks = v.reshape(v.shape[:-1] + (-1, 32))
    amax = np.abs(blocks).max(-1, keepdims=True)
    byte = np.maximum(np.where(amax > 0, np.frexp(amax)[1] - 1 + 127, 0) - down, 1)
    scale = np.exp2(byte - 127.0)
    codes = (blocks / scale).astype(np.float32).astype(dtype).astype(np.float64)
    return np.moveaxis((codes * scale).reshape(v.shape), -1, axis)


WIDE = False


def mx_kscale(k):
    if not WIDE:
        return np.ones(k)
    levels = np.array([10, -10, 5, -5, 0])
    if k % 512:
        return np.exp2(np.random.permutation(np.resize(levels, k // 32))).repeat(32)
    a = np.empty((k // 512, 16))
    for p in range(k // 512):
        a[p, :8] = np.random.permutation(np.resize(levels, 8))
        for g in range(8):
            far = levels[np.abs(levels - a[p, g]) >= 10]
            a[p, g + 8] = far[np.random.randint(len(far))]
    return np.exp2(a.ravel()).repeat(32)


def f64(x):
    return np.asarray(x).astype(np.float64)


def striped(idx):
    return np.tile(np.asarray(idx).reshape(-1, 16).T, (8, 1)).astype(np.uint16)


def unstriped(offs):
    return offs[:16].T.reshape(-1).astype(np.int64)


E2M1 = np.array([0.0, 0.5, 1.0, 1.5, 2.0, 3.0, 4.0, 6.0, -0.0, -0.5, -1.0, -1.5, -2.0, -3.0, -4.0, -6.0])


def pack_weight(w, fmt):
    k, n = w.shape
    w = f64(np.asarray(w, np.float32).astype(ml_dtypes.bfloat16)).reshape(k // 32, 32, n)
    amax = np.abs(w).max(1)
    if fmt == "e4m3":
        byte = np.frexp(amax)[1] - 1 + 127 - 7
    else:
        mant, ex = np.frexp(amax / 6.0)
        byte = np.where(mant > 0.5, ex, ex - 1) + 127
    byte = np.clip(np.where(amax > 0, byte, 1), 1, 254)
    scaled = (w * np.exp2(127.0 - byte)[:, None, :]).reshape(k, n).astype(np.float32)
    by_word = np.ascontiguousarray(scaled.reshape(k // 512, 128, 4, n).transpose(0, 1, 3, 2))
    if fmt == "e4m3":
        words = by_word.astype(ml_dtypes.float8_e4m3fn).view(np.uint8)
    else:
        c = by_word.astype(ml_dtypes.float4_e2m1fn).view(np.uint8) & 0xF
        words = (c[..., 0::2] | (c[..., 1::2] << 4)).reshape(k // 512, 128, 2 * n)
    return np.ascontiguousarray(words), np.ascontiguousarray(byte.astype(np.uint8).reshape(k // 512, 16, n))


def unpack_weight(words, scales, fmt):
    g, _, n = scales.shape
    words = np.ascontiguousarray(words).reshape(g, 128, n, -1)
    if fmt == "e4m3":
        vals = words.view(ml_dtypes.float8_e4m3fn).astype(np.float64)
    else:
        nib = np.empty((g, 128, n, 4), np.uint8)
        nib[..., 0::2] = words & 0xF
        nib[..., 1::2] = words >> 4
        vals = E2M1[nib]
    vals = vals * np.repeat(np.exp2(scales.astype(np.float64) - 127.0), 8, axis=1)[..., None]
    return vals.transpose(0, 1, 3, 2).reshape(g * 512, n)


def bf(x):
    return np.asarray(x, np.float32).astype(ml_dtypes.bfloat16)


def planes(Y):
    r, m = Y.shape
    b = f64(bf(Y)).reshape(r // 32, 32, m)
    amax = np.abs(b).max(1)
    byte = np.clip(np.where(amax > 0, np.frexp(amax)[1] - 1 + 127 - 7, 1), 1, 254)
    codes = (b * np.exp2(127.0 - byte)[:, None, :]).reshape(r, m).astype(np.float32).astype(ml_dtypes.float8_e4m3fn).view(np.uint8)
    words = codes.reshape(r // 512, 128, 4, m).transpose(0, 1, 3, 2)
    return np.ascontiguousarray(words), np.ascontiguousarray(byte.astype(np.uint8).reshape(r // 512, 16, m))


D, T, I, J, U, M, N = 512, 2048, 512, 512, 1024, 512, 64


def setup_inputs():
    n = np.random.standard_normal
    idx = np.random.permutation(T)[:I]
    idx2 = np.random.permutation(U)[:J]
    idx3 = np.random.permutation(M)[:N]
    fd = mx_kscale(D)
    keysp = pack_weight(n((D, T)) / fd[:, None], "e2m1")
    return {
        "keys_words": keysp[0],
        "keys_scales": keysp[1],
        "notes": (n((D, U)) * 1.0 / np.sqrt(D) * fd[:, None]).astype(np.float32),
        "old": (1.0 * n((I, M))).astype(np.float32),
        "offs": striped(idx),
        "offs2": striped(idx2),
        "offs3": striped(idx3),
    }


def reference(keys_words, keys_scales, notes, old, offs, offs2, offs3):
    idx = unstriped(offs)
    idx2 = unstriped(offs2)
    idx3 = unstriped(offs3)
    keysu = unpack_weight(keys_words, keys_scales, "e2m1")
    keysidxg = keysu[:, idx]
    notesidx2q = mxq(f64(notes)[:, idx2], 0, "e4m3")
    g0 = keysidxg.T @ notesidx2q
    rb0 = g0.reshape(I, N, J // N).max(axis=2)
    gf = np.zeros((I, M))
    gf[:, idx3] = rb0
    y = f64(old) + gf
    words, scales = planes(y)
    return y, words, scales

@@ -1,0 +1,152 @@
+from contextlib import ExitStack
+
+import concourse.mybir as mybir
+
+D, T, I, J, U, M, N = 512, 2048, 512, 512, 1024, 512, 64
+FLOPS = 2 * D * I * J
+
+F32 = mybir.dt.float32
+BF16 = mybir.dt.bfloat16
+I32 = mybir.dt.int32
+U32 = mybir.dt.uint32
+U16 = mybir.dt.uint16
+U8 = mybir.dt.uint8
+FP8X4 = mybir.dt.float8_e4m3fn_x4
+FP4X4 = mybir.dt.float4_e2m1fn_x4
+COPY = mybir.ActivationFunctionType.Copy
+ADD = mybir.AluOpType.add
+MAX = mybir.AluOpType.max
+AXIS_X = mybir.AxisListType.X
+
+P = 128
+PACK = 4
+RUN = J // N
+HALF = 256
+V_COLS = 320
+
+
+def tile_attend_tab_plain_runsput_pl_kernel(tc, keys_words, keys_scales, notes, old, offs, offs2, offs3, out_0, out_1, out_2):
+    nc = tc.nc
+    with ExitStack() as ctx:
+        held = ctx.enter_context(tc.tile_pool(name="held", bufs=1))
+        psum = ctx.enter_context(tc.psum_pool(name="psum", bufs=1))
+
+        key_list = held.tile([P, I // 16], U16, name="key_list")
+        note_list = held.tile([P, J // 16], U16, name="note_list")
+        run_list = held.tile([P, N // 16], U16, name="run_list")
+        pool_words = held.tile([P, T], U16, name="pool_words", align_bytes=64)
+        pool_scales = held.tile([P, T], U8, name="pool_scales", align_bytes=64)
+        note_rows = [held.tile([P, U], F32, name="note_rows%d" % t, align_bytes=64) for t in range(PACK)]
+        old_rows = held.tile([P, PACK, M], F32, name="old_rows", align_bytes=64)
+        placed = [held.tile([P, M], F32, name="placed%d" % t, align_bytes=64) for t in range(PACK)]
+
+        nc.gpsimd.memset(pool_scales[:].bitcast(I32), 0)
+        for t in range(PACK):
+            nc.gpsimd.memset(placed[t][:], 0.0)
+
+        notes_dealt = notes.rearrange("(p t) u -> p t u", t=PACK)
+        nc.sync.dma_start(note_list[:], offs2)
+        nc.sync.dma_start(note_rows[0][:], notes_dealt[:, 0, :])
+        nc.sync.dma_start(key_list[:], offs)
+        nc.sync.dma_start(pool_words[:].bitcast(I32), keys_words[0].bitcast(I32))
+        for q in range(4):
+            nc.scalar.dma_start(
+                pool_scales[32 * q : 32 * q + 4, :].bitcast(I32),
+                keys_scales[0, 4 * q : 4 * q + 4, :].bitcast(I32),
+            )
+        for t in range(1, PACK):
+            nc.sync.dma_start(note_rows[t][:], notes_dealt[:, t, :])
+        nc.sync.dma_start(run_list[:], offs3)
+        nc.sync.dma_start(old_rows[:], old.rearrange("(p t) m -> p t m", t=PACK))
+
+        picked_words = held.tile([P, I], U16, name="picked_words", align_bytes=64)
+        key_words = held.tile([P, PACK, P], U16, name="key_words", align_bytes=64)
+        key_scales = held.tile([P, PACK, P], U8, name="key_scales", align_bytes=64)
+        nc.vector.tensor_copy(key_scales[:].rearrange("p t s -> p s t"), pool_scales[:].indirect(key_list[:]))
+        nc.vector.tensor_copy(picked_words[:], pool_words[:].indirect(key_list[:]))
+        nc.vector.tensor_copy(key_words[:], picked_words[:].rearrange("p (s t) -> p t s", t=PACK))
+
+        picked_notes = held.tile([P, PACK, J], BF16, name="picked_notes", align_bytes=64)
+        nc.scalar.activation(picked_notes[:, 0, :], note_rows[0][:].indirect(note_list[:]), COPY)
+        for t in range(1, PACK):
+            nc.vector.tensor_copy(picked_notes[:, t, :HALF], note_rows[t][:].indirect(note_list[:, : HALF // 16]))
+            nc.scalar.activation(picked_notes[:, t, HALF:], note_rows[t][:].indirect(note_list[:, HALF // 16 :]), COPY)
+
+        woven_notes = held.tile([P, J, PACK], BF16, name="woven_notes", align_bytes=64)
+        note_words = held.tile([P, J], U32, name="note_words", align_bytes=64)
+        note_scales = held.tile([P, J], U8, name="note_scales", align_bytes=64)
+
+        def weave(copy, dst, src, a, b):
+            copy(
+                dst[:, a:b, :].rearrange("p (c i) t -> p c t i", i=4),
+                src[:, :, a:b].rearrange("p t (c i) -> p c t i", i=4),
+            )
+
+        weave(nc.vector.tensor_copy, woven_notes, picked_notes, 0, HALF)
+        weave(nc.scalar.copy, woven_notes, picked_notes, V_COLS, J)
+        weave(nc.vector.tensor_copy, woven_notes, picked_notes, HALF, V_COLS)
+        for h in range(2):
+            cols = slice(h * HALF, (h + 1) * HALF)
+            nc.vector.quantize_mx(
+                out=note_words[:, cols].bitcast(FP8X4),
+                scales=note_scales[:, cols],
+                in_=woven_notes[:, cols, :].rearrange("p c t -> p (c t)"),
+            )
+
+        banks = {}
+        for t in range(PACK):
+            for h in range(2):
+                cols = slice(h * HALF, (h + 1) * HALF)
+                banks[t, h] = psum.tile([P, HALF], F32, name="bank%d%d" % (t, h))
+                nc.tensor.matmul_mx(
+                    out=banks[t, h][:],
+                    lhsT=key_words[:, t, :].bitcast(FP4X4),
+                    lhsT_scale=key_scales[:, t, :],
+                    rhs=note_words[:, cols].bitcast(FP8X4),
+                    rhs_scale=note_scales[:, cols],
+                    start=True,
+                    stop=True,
+                )
+
+        result = held.tile([P, PACK, M], F32, name="result", align_bytes=64)
+        out_dealt = out_0.rearrange("(p t) m -> p t m", t=PACK)
+        for t in range(PACK):
+            run_max = held.tile([P, N], F32, name="run_max%d" % t)
+            for h in range(2):
+                nc.vector.tensor_reduce(
+                    run_max[:, h * (N // 2) : (h + 1) * (N // 2)],
+                    banks[t, h][:].rearrange("p (n r) -> p n r", r=RUN),
+                    AXIS_X,
+                    MAX,
+                )
+            nc.scalar.activation(placed[t][:].indirect(run_list[:]), run_max[:], COPY)
+
+        woven_result = held.tile([P, M, PACK], BF16, name="woven_result", align_bytes=64)
+        result_words = held.tile([P, M], U32, name="result_words", align_bytes=64)
+        result_scales = held.tile([P, M], U8, name="result_scales", align_bytes=64)
+        nc.gpsimd.tensor_tensor(result[:, 0, :], old_rows[:, 0, :], placed[0][:], ADD)
+        nc.sync.dma_start(out_dealt[:, 0, :], result[:, 0, :])
+        nc.vector.tensor_tensor(result[:, 1, :], old_rows[:, 1, :], placed[1][:], ADD)
+        nc.sync.dma_start(out_dealt[:, 1, :], result[:, 1, :])
+        for h in (1, 0):
+            cols = slice(h * HALF, (h + 1) * HALF)
+            for t in (2, 3):
+                nc.vector.tensor_tensor(result[:, t, cols], old_rows[:, t, cols], placed[t][:, cols], ADD)
+        nc.sync.dma_start(out_dealt[:, 2:, :], result[:, 2:, :])
+        weave(nc.scalar.copy, woven_result, result, HALF, M)
+        weave(nc.vector.tensor_copy, woven_result, result, 0, HALF)
+        words_out = out_1[0].rearrange("p c t -> p (c t)").bitcast(I32)
+        for h in range(2):
+            cols = slice(h * HALF, (h + 1) * HALF)
+            nc.vector.quantize_mx(
+                out=result_words[:, cols].bitcast(FP8X4),
+                scales=result_scales[:, cols],
+                in_=woven_result[:, cols, :].rearrange("p c t -> p (c t)"),
+            )
+            nc.sync.dma_start(words_out[:, cols], result_words[:, cols].bitcast(I32))
+        for q in range(4):
+            queue = nc.scalar if q % 2 else nc.sync
+            queue.dma_start(
+                out_2[0, 4 * q : 4 * q + 4, :].bitcast(I32),
+                result_scales[32 * q : 32 * q + 4, :].bitcast(I32),
+            )

@@ -22,7 +22,6 @@ P = 128
 PACK = 4
 RUN = J // N
 HALF = 256
-V_COLS = 320
 
 
 def tile_attend_tab_plain_runsput_pl_kernel(tc, keys_words, keys_scales, notes, old, offs, offs2, offs3, out_0, out_1, out_2):
@@ -42,19 +41,22 @@ def tile_attend_tab_plain_runsput_pl_kernel(tc, keys_words, keys_scales, notes, 
 
         nc.gpsimd.memset(pool_scales[:].bitcast(I32), 0)
         for t in range(PACK):
-            nc.gpsimd.memset(placed[t][:], 0.0)
+            nc.vector.memset(placed[t][:], 0.0)
+
+        warm = held.tile([P, 2], F32, name="warm")
+        nc.vector.memset(warm[:, 0:1], 0.0)
+        nc.scalar.activation(warm[:, 1:2], warm[:, 0:1], COPY)
 
         notes_dealt = notes.rearrange("(p t) u -> p t u", t=PACK)
-        nc.sync.dma_start(note_list[:], offs2)
-        nc.sync.dma_start(note_rows[0][:], notes_dealt[:, 0, :])
         nc.sync.dma_start(key_list[:], offs)
         nc.sync.dma_start(pool_words[:].bitcast(I32), keys_words[0].bitcast(I32))
         for q in range(4):
-            nc.scalar.dma_start(
+            nc.sync.dma_start(
                 pool_scales[32 * q : 32 * q + 4, :].bitcast(I32),
                 keys_scales[0, 4 * q : 4 * q + 4, :].bitcast(I32),
             )
-        for t in range(1, PACK):
+        nc.sync.dma_start(note_list[:], offs2)
+        for t in range(PACK):
             nc.sync.dma_start(note_rows[t][:], notes_dealt[:, t, :])
         nc.sync.dma_start(run_list[:], offs3)
         nc.sync.dma_start(old_rows[:], old.rearrange("(p t) m -> p t m", t=PACK))
@@ -62,44 +64,53 @@ def tile_attend_tab_plain_runsput_pl_kernel(tc, keys_words, keys_scales, notes, 
         picked_words = held.tile([P, I], U16, name="picked_words", align_bytes=64)
         key_words = held.tile([P, PACK, P], U16, name="key_words", align_bytes=64)
         key_scales = held.tile([P, PACK, P], U8, name="key_scales", align_bytes=64)
-        nc.vector.tensor_copy(key_scales[:].rearrange("p t s -> p s t"), pool_scales[:].indirect(key_list[:]))
         nc.vector.tensor_copy(picked_words[:], pool_words[:].indirect(key_list[:]))
+        nc.vector.tensor_copy(key_scales[:].rearrange("p t s -> p s t"), pool_scales[:].indirect(key_list[:]))
         nc.vector.tensor_copy(key_words[:], picked_words[:].rearrange("p (s t) -> p t s", t=PACK))
 
-        picked_notes = held.tile([P, PACK, J], BF16, name="picked_notes", align_bytes=64)
-        nc.scalar.activation(picked_notes[:, 0, :], note_rows[0][:].indirect(note_list[:]), COPY)
-        for t in range(1, PACK):
-            nc.vector.tensor_copy(picked_notes[:, t, :HALF], note_rows[t][:].indirect(note_list[:, : HALF // 16]))
-            nc.scalar.activation(picked_notes[:, t, HALF:], note_rows[t][:].indirect(note_list[:, HALF // 16 :]), COPY)
-
-        woven_notes = held.tile([P, J, PACK], BF16, name="woven_notes", align_bytes=64)
+        picked = {}
+        for pair in range(2):
+            for h in range(2):
+                picked[pair, h] = held.tile([P, 2, HALF], BF16, name="picked%d%d" % (pair, h), align_bytes=64)
+        woven_notes = [held.tile([P, HALF, PACK], BF16, name="woven_notes%d" % h, align_bytes=64) for h in range(2)]
         note_words = held.tile([P, J], U32, name="note_words", align_bytes=64)
         note_scales = held.tile([P, J], U8, name="note_scales", align_bytes=64)
 
-        def weave(copy, dst, src, a, b):
+        def weave(copy, dst, src):
             copy(
-                dst[:, a:b, :].rearrange("p (c i) t -> p c t i", i=4),
-                src[:, :, a:b].rearrange("p t (c i) -> p c t i", i=4),
+                dst.rearrange("p (c i) t -> p c t i", i=4),
+                src.rearrange("p t (c i) -> p c t i", i=4),
             )
 
-        weave(nc.vector.tensor_copy, woven_notes, picked_notes, 0, HALF)
-        weave(nc.scalar.copy, woven_notes, picked_notes, V_COLS, J)
-        weave(nc.vector.tensor_copy, woven_notes, picked_notes, HALF, V_COLS)
+        for pair in range(2):
+            for e in range(2):
+                for h in range(2):
+                    window = note_rows[2 * pair + e][:].indirect(note_list[:, h * HALF // 16 : (h + 1) * HALF // 16])
+                    if e == 1 and h == 0:
+                        nc.vector.tensor_copy(picked[pair, h][:, e, :], window)
+                    else:
+                        nc.scalar.activation(picked[pair, h][:, e, :], window, COPY)
+            for h in range(2):
+                copy = nc.scalar.copy if pair == 1 and h == 1 else nc.vector.tensor_copy
+                weave(copy, woven_notes[h][:, :, 2 * pair : 2 * pair + 2], picked[pair, h][:])
         for h in range(2):
             cols = slice(h * HALF, (h + 1) * HALF)
             nc.vector.quantize_mx(
                 out=note_words[:, cols].bitcast(FP8X4),
                 scales=note_scales[:, cols],
-                in_=woven_notes[:, cols, :].rearrange("p c t -> p (c t)"),
+                in_=woven_notes[h][:].rearrange("p c t -> p (c t)"),
             )
 
-        banks = {}
+        result = [held.tile([P, PACK, HALF], F32, name="result%d" % h, align_bytes=64) for h in range(2)]
+        out_dealt = out_0.rearrange("(p t) m -> p t m", t=PACK)
         for t in range(PACK):
-            for h in range(2):
-                cols = slice(h * HALF, (h + 1) * HALF)
-                banks[t, h] = psum.tile([P, HALF], F32, name="bank%d%d" % (t, h))
+            run_max = held.tile([P, N], F32, name="run_max%d" % t)
+            width = HALF
+            for j0 in range(0, J, width):
+                cols = slice(j0, j0 + width)
+                bank = psum.tile([P, width], F32, name="bank%d_%d" % (t, j0))
                 nc.tensor.matmul_mx(
-                    out=banks[t, h][:],
+                    out=bank[:],
                     lhsT=key_words[:, t, :].bitcast(FP4X4),
                     lhsT_scale=key_scales[:, t, :],
                     rhs=note_words[:, cols].bitcast(FP8X4),
@@ -107,15 +118,9 @@ def tile_attend_tab_plain_runsput_pl_kernel(tc, keys_words, keys_scales, notes, 
                     start=True,
                     stop=True,
                 )
-
-        result = held.tile([P, PACK, M], F32, name="result", align_bytes=64)
-        out_dealt = out_0.rearrange("(p t) m -> p t m", t=PACK)
-        for t in range(PACK):
-            run_max = held.tile([P, N], F32, name="run_max%d" % t)
-            for h in range(2):
                 nc.vector.tensor_reduce(
-                    run_max[:, h * (N // 2) : (h + 1) * (N // 2)],
-                    banks[t, h][:].rearrange("p (n r) -> p n r", r=RUN),
+                    run_max[:, j0 // RUN : (j0 + width) // RUN],
+                    bank[:].rearrange("p (n r) -> p n r", r=RUN),
                     AXIS_X,
                     MAX,
                 )
@@ -124,19 +129,16 @@ def tile_attend_tab_plain_runsput_pl_kernel(tc, keys_words, keys_scales, notes, 
         woven_result = held.tile([P, M, PACK], BF16, name="woven_result", align_bytes=64)
         result_words = held.tile([P, M], U32, name="result_words", align_bytes=64)
         result_scales = held.tile([P, M], U8, name="result_scales", align_bytes=64)
-        nc.gpsimd.tensor_tensor(result[:, 0, :], old_rows[:, 0, :], placed[0][:], ADD)
-        nc.sync.dma_start(out_dealt[:, 0, :], result[:, 0, :])
-        nc.vector.tensor_tensor(result[:, 1, :], old_rows[:, 1, :], placed[1][:], ADD)
-        nc.sync.dma_start(out_dealt[:, 1, :], result[:, 1, :])
         for h in (1, 0):
             cols = slice(h * HALF, (h + 1) * HALF)
-            for t in (2, 3):
-                nc.vector.tensor_tensor(result[:, t, cols], old_rows[:, t, cols], placed[t][:, cols], ADD)
-        nc.sync.dma_start(out_dealt[:, 2:, :], result[:, 2:, :])
-        weave(nc.scalar.copy, woven_result, result, HALF, M)
-        weave(nc.vector.tensor_copy, woven_result, result, 0, HALF)
+            for t in range(PACK):
+                engine = nc.gpsimd if t == 0 else nc.vector
+                engine.tensor_tensor(result[h][:, t, :], old_rows[:, t, cols], placed[t][:, cols], ADD)
+                if t % 2:
+                    nc.sync.dma_start(out_dealt[:, t - 1 : t + 1, cols], result[h][:, t - 1 : t + 1, :])
+            weave(nc.scalar.copy if h else nc.vector.tensor_copy, woven_result[:, cols, :], result[h][:])
         words_out = out_1[0].rearrange("p c t -> p (c t)").bitcast(I32)
-        for h in range(2):
+        for h in (1, 0):
             cols = slice(h * HALF, (h + 1) * HALF)
             nc.vector.quantize_mx(
                 out=result_words[:, cols].bitcast(FP8X4),

@@ -49,13 +49,13 @@ def tile_attend_tab_plain_runsput_pl_kernel(tc, keys_words, keys_scales, notes, 
 
         notes_dealt = notes.rearrange("(p t) u -> p t u", t=PACK)
         nc.sync.dma_start(key_list[:], offs)
-        nc.sync.dma_start(pool_words[:].bitcast(I32), keys_words[0].bitcast(I32))
+        nc.sync.dma_start(note_list[:], offs2)
         for q in range(4):
             nc.sync.dma_start(
                 pool_scales[32 * q : 32 * q + 4, :].bitcast(I32),
                 keys_scales[0, 4 * q : 4 * q + 4, :].bitcast(I32),
             )
-        nc.sync.dma_start(note_list[:], offs2)
+        nc.sync.dma_start(pool_words[:].bitcast(I32), keys_words[0].bitcast(I32))
         for t in range(PACK):
             nc.sync.dma_start(note_rows[t][:], notes_dealt[:, t, :])
         nc.sync.dma_start(run_list[:], offs3)
@@ -64,14 +64,10 @@ def tile_attend_tab_plain_runsput_pl_kernel(tc, keys_words, keys_scales, notes, 
         picked_words = held.tile([P, I], U16, name="picked_words", align_bytes=64)
         key_words = held.tile([P, PACK, P], U16, name="key_words", align_bytes=64)
         key_scales = held.tile([P, PACK, P], U8, name="key_scales", align_bytes=64)
-        nc.vector.tensor_copy(picked_words[:], pool_words[:].indirect(key_list[:]))
         nc.vector.tensor_copy(key_scales[:].rearrange("p t s -> p s t"), pool_scales[:].indirect(key_list[:]))
+        nc.vector.tensor_copy(picked_words[:], pool_words[:].indirect(key_list[:]))
         nc.vector.tensor_copy(key_words[:], picked_words[:].rearrange("p (s t) -> p t s", t=PACK))
 
-        picked = {}
-        for pair in range(2):
-            for h in range(2):
-                picked[pair, h] = held.tile([P, 2, HALF], BF16, name="picked%d%d" % (pair, h), align_bytes=64)
         woven_notes = [held.tile([P, HALF, PACK], BF16, name="woven_notes%d" % h, align_bytes=64) for h in range(2)]
         note_words = held.tile([P, J], U32, name="note_words", align_bytes=64)
         note_scales = held.tile([P, J], U8, name="note_scales", align_bytes=64)
@@ -82,26 +78,28 @@ def tile_attend_tab_plain_runsput_pl_kernel(tc, keys_words, keys_scales, notes, 
                 src.rearrange("p t (c i) -> p c t i", i=4),
             )
 
+        def listed(t, a, b):
+            return note_rows[t][:].indirect(note_list[:, a // 16 : b // 16])
+
         for pair in range(2):
+            width = P if pair else HALF
+            starts = range(0, HALF, width)
+            picked = {j0: held.tile([P, 2, width], BF16, name="picked%d_%d" % (pair, j0), align_bytes=64) for j0 in starts}
             for e in range(2):
-                for h in range(2):
-                    window = note_rows[2 * pair + e][:].indirect(note_list[:, h * HALF // 16 : (h + 1) * HALF // 16])
-                    if e == 1 and h == 0:
-                        nc.vector.tensor_copy(picked[pair, h][:, e, :], window)
-                    else:
-                        nc.scalar.activation(picked[pair, h][:, e, :], window, COPY)
-            for h in range(2):
-                copy = nc.scalar.copy if pair == 1 and h == 1 else nc.vector.tensor_copy
-                weave(copy, woven_notes[h][:, :, 2 * pair : 2 * pair + 2], picked[pair, h][:])
-        for h in range(2):
-            cols = slice(h * HALF, (h + 1) * HALF)
+                t = 2 * pair + e
+                for j0 in starts:
+                    nc.vector.tensor_copy(woven_notes[0][:, j0 : j0 + width, t], listed(t, j0, j0 + width))
+                    nc.scalar.activation(picked[j0][:, e, :], listed(t, HALF + j0, HALF + j0 + width), COPY)
+            for j0 in starts:
+                weave(nc.scalar.copy, woven_notes[1][:, j0 : j0 + width, 2 * pair : 2 * pair + 2], picked[j0][:])
+        for h, a, b in ((0, 0, P), (0, P, HALF), (1, 0, HALF)):
+            cols = slice(h * HALF + a, h * HALF + b)
             nc.vector.quantize_mx(
                 out=note_words[:, cols].bitcast(FP8X4),
                 scales=note_scales[:, cols],
-                in_=woven_notes[h][:].rearrange("p c t -> p (c t)"),
+                in_=woven_notes[h][:, a:b, :].rearrange("p c t -> p (c t)"),
             )
 
-        result = [held.tile([P, PACK, HALF], F32, name="result%d" % h, align_bytes=64) for h in range(2)]
         out_dealt = out_0.rearrange("(p t) m -> p t m", t=PACK)
         for t in range(PACK):
             run_max = held.tile([P, N], F32, name="run_max%d" % t)
@@ -126,24 +124,32 @@ def tile_attend_tab_plain_runsput_pl_kernel(tc, keys_words, keys_scales, notes, 
                 )
             nc.scalar.activation(placed[t][:].indirect(run_list[:]), run_max[:], COPY)
 
-        woven_result = held.tile([P, M, PACK], BF16, name="woven_result", align_bytes=64)
+        woven_result = [held.tile([P, HALF, PACK], BF16, name="woven_result%d" % h, align_bytes=64) for h in range(2)]
         result_words = held.tile([P, M], U32, name="result_words", align_bytes=64)
         result_scales = held.tile([P, M], U8, name="result_scales", align_bytes=64)
-        for h in (1, 0):
-            cols = slice(h * HALF, (h + 1) * HALF)
-            for t in range(PACK):
-                engine = nc.gpsimd if t == 0 else nc.vector
-                engine.tensor_tensor(result[h][:, t, :], old_rows[:, t, cols], placed[t][:, cols], ADD)
-                if t % 2:
-                    nc.sync.dma_start(out_dealt[:, t - 1 : t + 1, cols], result[h][:, t - 1 : t + 1, :])
-            weave(nc.scalar.copy if h else nc.vector.tensor_copy, woven_result[:, cols, :], result[h][:])
+        for pair in range(2):
+            result = [held.tile([P, 2, HALF], F32, name="result%d%d" % (pair, h), align_bytes=64) for h in range(2)]
+            for h in range(2):
+                cols = slice(h * HALF, (h + 1) * HALF)
+                for e in range(2):
+                    t = 2 * pair + e
+                    nc.vector.tensor_tensor(result[h][:, e, :], old_rows[:, t, cols], placed[t][:, cols], ADD)
+            for h in range(2):
+                cols = slice(h * HALF, (h + 1) * HALF)
+                nc.sync.dma_start(out_dealt[:, 2 * pair : 2 * pair + 2, cols], result[h][:])
+                split = (0, 0, HALF, P)[2 * pair + h]
+                places = slice(2 * pair, 2 * pair + 2)
+                if split > 0:
+                    weave(nc.vector.tensor_copy, woven_result[h][:, :split, places], result[h][:, :, :split])
+                if split < HALF:
+                    weave(nc.scalar.copy, woven_result[h][:, split:, places], result[h][:, :, split:])
         words_out = out_1[0].rearrange("p c t -> p (c t)").bitcast(I32)
-        for h in (1, 0):
+        for h in range(2):
             cols = slice(h * HALF, (h + 1) * HALF)
             nc.vector.quantize_mx(
                 out=result_words[:, cols].bitcast(FP8X4),
                 scales=result_scales[:, cols],
-                in_=woven_result[:, cols, :].rearrange("p c t -> p (c t)"),
+                in_=woven_result[h][:].rearrange("p c t -> p (c t)"),
             )
             nc.sync.dma_start(words_out[:, cols], result_words[:, cols].bitcast(I32))
         for q in range(4):

@@ -40,23 +40,23 @@ def tile_attend_tab_plain_runsput_pl_kernel(tc, keys_words, keys_scales, notes, 
         placed = [held.tile([P, M], F32, name="placed%d" % t, align_bytes=64) for t in range(PACK)]
 
         nc.gpsimd.memset(pool_scales[:].bitcast(I32), 0)
-        for t in range(PACK):
-            nc.vector.memset(placed[t][:], 0.0)
-
         warm = held.tile([P, 2], F32, name="warm")
-        nc.vector.memset(warm[:, 0:1], 0.0)
+        nc.gpsimd.memset(warm[:, 0:1], 0.0)
         nc.scalar.activation(warm[:, 1:2], warm[:, 0:1], COPY)
+        for t in range(PACK):
+            nc.gpsimd.memset(placed[t][:], 0.0)
 
         notes_dealt = notes.rearrange("(p t) u -> p t u", t=PACK)
         nc.sync.dma_start(key_list[:], offs)
+        nc.sync.dma_start(pool_words[:].bitcast(I32), keys_words[0].bitcast(I32))
         nc.sync.dma_start(note_list[:], offs2)
+        nc.sync.dma_start(note_rows[0][:], notes_dealt[:, 0, :])
         for q in range(4):
             nc.sync.dma_start(
                 pool_scales[32 * q : 32 * q + 4, :].bitcast(I32),
                 keys_scales[0, 4 * q : 4 * q + 4, :].bitcast(I32),
             )
-        nc.sync.dma_start(pool_words[:].bitcast(I32), keys_words[0].bitcast(I32))
-        for t in range(PACK):
+        for t in range(1, PACK):
             nc.sync.dma_start(note_rows[t][:], notes_dealt[:, t, :])
         nc.sync.dma_start(run_list[:], offs3)
         nc.sync.dma_start(old_rows[:], old.rearrange("(p t) m -> p t m", t=PACK))
@@ -64,34 +64,35 @@ def tile_attend_tab_plain_runsput_pl_kernel(tc, keys_words, keys_scales, notes, 
         picked_words = held.tile([P, I], U16, name="picked_words", align_bytes=64)
         key_words = held.tile([P, PACK, P], U16, name="key_words", align_bytes=64)
         key_scales = held.tile([P, PACK, P], U8, name="key_scales", align_bytes=64)
-        nc.vector.tensor_copy(key_scales[:].rearrange("p t s -> p s t"), pool_scales[:].indirect(key_list[:]))
         nc.vector.tensor_copy(picked_words[:], pool_words[:].indirect(key_list[:]))
         nc.vector.tensor_copy(key_words[:], picked_words[:].rearrange("p (s t) -> p t s", t=PACK))
+        nc.vector.tensor_copy(key_scales[:].rearrange("p t s -> p s t"), pool_scales[:].indirect(key_list[:]))
 
         woven_notes = [held.tile([P, HALF, PACK], BF16, name="woven_notes%d" % h, align_bytes=64) for h in range(2)]
         note_words = held.tile([P, J], U32, name="note_words", align_bytes=64)
         note_scales = held.tile([P, J], U8, name="note_scales", align_bytes=64)
 
         def weave(copy, dst, src):
-            copy(
-                dst.rearrange("p (c i) t -> p c t i", i=4),
-                src.rearrange("p t (c i) -> p c t i", i=4),
-            )
+            copy(dst, src.rearrange("p t c -> p c t"))
 
         def listed(t, a, b):
             return note_rows[t][:].indirect(note_list[:, a // 16 : b // 16])
 
         for pair in range(2):
             width = P if pair else HALF
-            starts = range(0, HALF, width)
+            starts = range(0, J, width)
             picked = {j0: held.tile([P, 2, width], BF16, name="picked%d_%d" % (pair, j0), align_bytes=64) for j0 in starts}
             for e in range(2):
-                t = 2 * pair + e
                 for j0 in starts:
-                    nc.vector.tensor_copy(woven_notes[0][:, j0 : j0 + width, t], listed(t, j0, j0 + width))
-                    nc.scalar.activation(picked[j0][:, e, :], listed(t, HALF + j0, HALF + j0 + width), COPY)
+                    window = listed(2 * pair + e, j0, j0 + width)
+                    if e == 1 and j0 < HALF:
+                        nc.vector.tensor_copy(picked[j0][:, e, :], window)
+                    else:
+                        nc.scalar.activation(picked[j0][:, e, :], window, COPY)
             for j0 in starts:
-                weave(nc.scalar.copy, woven_notes[1][:, j0 : j0 + width, 2 * pair : 2 * pair + 2], picked[j0][:])
+                h, c0 = divmod(j0, HALF)
+                copy = nc.scalar.copy if pair == 1 and h == 1 else nc.vector.tensor_copy
+                weave(copy, woven_notes[h][:, c0 : c0 + width, 2 * pair : 2 * pair + 2], picked[j0][:])
         for h, a, b in ((0, 0, P), (0, P, HALF), (1, 0, HALF)):
             cols = slice(h * HALF + a, h * HALF + b)
             nc.vector.quantize_mx(

from contextlib import ExitStack

import concourse.mybir as mybir

D, T, I, J, U, M, N = 512, 2048, 512, 512, 1024, 512, 64
FLOPS = 2 * D * I * J

F32 = mybir.dt.float32
BF16 = mybir.dt.bfloat16
I32 = mybir.dt.int32
U32 = mybir.dt.uint32
U16 = mybir.dt.uint16
U8 = mybir.dt.uint8
FP8X4 = mybir.dt.float8_e4m3fn_x4
FP4X4 = mybir.dt.float4_e2m1fn_x4
COPY = mybir.ActivationFunctionType.Copy
ADD = mybir.AluOpType.add
MAX = mybir.AluOpType.max
AXIS_X = mybir.AxisListType.X

P = 128
PACK = 4
RUN = J // N
HALF = 256


def tile_attend_tab_plain_runsput_pl_kernel(tc, keys_words, keys_scales, notes, old, offs, offs2, offs3, out_0, out_1, out_2):
    nc = tc.nc
    with ExitStack() as ctx:
        held = ctx.enter_context(tc.tile_pool(name="held", bufs=1))
        psum = ctx.enter_context(tc.psum_pool(name="psum", bufs=1))

        key_list = held.tile([P, I // 16], U16, name="key_list")
        note_list = held.tile([P, J // 16], U16, name="note_list")
        run_list = held.tile([P, N // 16], U16, name="run_list")
        pool_words = held.tile([P, T], U16, name="pool_words", align_bytes=64)
        pool_scales = held.tile([P, T], U8, name="pool_scales", align_bytes=64)
        note_rows = [held.tile([P, U], F32, name="note_rows%d" % t, align_bytes=64) for t in range(PACK)]
        old_rows = held.tile([P, PACK, M], F32, name="old_rows", align_bytes=64)
        placed = [held.tile([P, M], F32, name="placed%d" % t, align_bytes=64) for t in range(PACK)]

        nc.gpsimd.memset(pool_scales[:].bitcast(I32), 0)
        warm = held.tile([P, 2], F32, name="warm")
        nc.gpsimd.memset(warm[:, 0:1], 0.0)
        nc.scalar.activation(warm[:, 1:2], warm[:, 0:1], COPY)
        for t in range(PACK):
            nc.gpsimd.memset(placed[t][:], 0.0)

        notes_dealt = notes.rearrange("(p t) u -> p t u", t=PACK)
        nc.sync.dma_start(key_list[:], offs)
        nc.sync.dma_start(pool_words[:].bitcast(I32), keys_words[0].bitcast(I32))
        nc.sync.dma_start(note_list[:], offs2)
        nc.sync.dma_start(note_rows[0][:], notes_dealt[:, 0, :])
        for q in range(4):
            nc.sync.dma_start(
                pool_scales[32 * q : 32 * q + 4, :].bitcast(I32),
                keys_scales[0, 4 * q : 4 * q + 4, :].bitcast(I32),
            )
        for t in range(1, PACK):
            nc.sync.dma_start(note_rows[t][:], notes_dealt[:, t, :])
        nc.sync.dma_start(run_list[:], offs3)
        nc.sync.dma_start(old_rows[:], old.rearrange("(p t) m -> p t m", t=PACK))

        picked_words = held.tile([P, I], U16, name="picked_words", align_bytes=64)
        key_words = held.tile([P, PACK, P], U16, name="key_words", align_bytes=64)
        key_scales = held.tile([P, PACK, P], U8, name="key_scales", align_bytes=64)
        nc.vector.tensor_copy(picked_words[:], pool_words[:].indirect(key_list[:]))
        nc.vector.tensor_copy(key_words[:], picked_words[:].rearrange("p (s t) -> p t s", t=PACK))
        nc.vector.tensor_copy(key_scales[:].rearrange("p t s -> p s t"), pool_scales[:].indirect(key_list[:]))

        woven_notes = [held.tile([P, HALF, PACK], BF16, name="woven_notes%d" % h, align_bytes=64) for h in range(2)]
        note_words = held.tile([P, J], U32, name="note_words", align_bytes=64)
        note_scales = held.tile([P, J], U8, name="note_scales", align_bytes=64)

        def weave(copy, dst, src):
            copy(dst, src.rearrange("p t c -> p c t"))

        def listed(t, a, b):
            return note_rows[t][:].indirect(note_list[:, a // 16 : b // 16])

        for pair in range(2):
            width = P if pair else HALF
            starts = range(0, J, width)
            picked = {j0: held.tile([P, 2, width], BF16, name="picked%d_%d" % (pair, j0), align_bytes=64) for j0 in starts}
            for e in range(2):
                for j0 in starts:
                    window = listed(2 * pair + e, j0, j0 + width)
                    if e == 1 and j0 < HALF:
                        nc.vector.tensor_copy(picked[j0][:, e, :], window)
                    else:
                        nc.scalar.activation(picked[j0][:, e, :], window, COPY)
            for j0 in starts:
                h, c0 = divmod(j0, HALF)
                copy = nc.scalar.copy if pair == 1 and h == 1 else nc.vector.tensor_copy
                weave(copy, woven_notes[h][:, c0 : c0 + width, 2 * pair : 2 * pair + 2], picked[j0][:])
        for h, a, b in ((0, 0, P), (0, P, HALF), (1, 0, HALF)):
            cols = slice(h * HALF + a, h * HALF + b)
            nc.vector.quantize_mx(
                out=note_words[:, cols].bitcast(FP8X4),
                scales=note_scales[:, cols],
                in_=woven_notes[h][:, a:b, :].rearrange("p c t -> p (c t)"),
            )

        out_dealt = out_0.rearrange("(p t) m -> p t m", t=PACK)
        for t in range(PACK):
            run_max = held.tile([P, N], F32, name="run_max%d" % t)
            width = HALF
            for j0 in range(0, J, width):
                cols = slice(j0, j0 + width)
                bank = psum.tile([P, width], F32, name="bank%d_%d" % (t, j0))
                nc.tensor.matmul_mx(
                    out=bank[:],
                    lhsT=key_words[:, t, :].bitcast(FP4X4),
                    lhsT_scale=key_scales[:, t, :],
                    rhs=note_words[:, cols].bitcast(FP8X4),
                    rhs_scale=note_scales[:, cols],
                    start=True,
                    stop=True,
                )
                nc.vector.tensor_reduce(
                    run_max[:, j0 // RUN : (j0 + width) // RUN],
                    bank[:].rearrange("p (n r) -> p n r", r=RUN),
                    AXIS_X,
                    MAX,
                )
            nc.scalar.activation(placed[t][:].indirect(run_list[:]), run_max[:], COPY)

        woven_result = [held.tile([P, HALF, PACK], BF16, name="woven_result%d" % h, align_bytes=64) for h in range(2)]
        result_words = held.tile([P, M], U32, name="result_words", align_bytes=64)
        result_scales = held.tile([P, M], U8, name="result_scales", align_bytes=64)
        for pair in range(2):
            result = [held.tile([P, 2, HALF], F32, name="result%d%d" % (pair, h), align_bytes=64) for h in range(2)]
            for h in range(2):
                cols = slice(h * HALF, (h + 1) * HALF)
                for e in range(2):
                    t = 2 * pair + e
                    nc.vector.tensor_tensor(result[h][:, e, :], old_rows[:, t, cols], placed[t][:, cols], ADD)
            for h in range(2):
                cols = slice(h * HALF, (h + 1) * HALF)
                nc.sync.dma_start(out_dealt[:, 2 * pair : 2 * pair + 2, cols], result[h][:])
                split = (0, 0, HALF, P)[2 * pair + h]
                places = slice(2 * pair, 2 * pair + 2)
                if split > 0:
                    weave(nc.vector.tensor_copy, woven_result[h][:, :split, places], result[h][:, :, :split])
                if split < HALF:
                    weave(nc.scalar.copy, woven_result[h][:, split:, places], result[h][:, :, split:])
        words_out = out_1[0].rearrange("p c t -> p (c t)").bitcast(I32)
        for h in range(2):
            cols = slice(h * HALF, (h + 1) * HALF)
            nc.vector.quantize_mx(
                out=result_words[:, cols].bitcast(FP8X4),
                scales=result_scales[:, cols],
                in_=woven_result[h][:].rearrange("p c t -> p (c t)"),
            )
            nc.sync.dma_start(words_out[:, cols], result_words[:, cols].bitcast(I32))
        for q in range(4):
            queue = nc.scalar if q % 2 else nc.sync
            queue.dma_start(
                out_2[0, 4 * q : 4 * q + 4, :].bitcast(I32),
                result_scales[32 * q : 32 * q + 4, :].bitcast(I32),
            )
